import numpy as np
import ml_dtypes

BF16 = ml_dtypes.bfloat16


def bf(x):
    return np.asarray(x, np.float32).astype(BF16)


def f32(x):
    return np.asarray(x, np.float32)


def f64(x):
    return np.asarray(x).astype(np.float64)


def striped(idx):
    return np.tile(idx.reshape(-1, 16).T, (8, 1))


S, K, M, N, V, D, H = 1024, 256, 512, 512, 256, 2, 256


def sigmoid(v):
    return 1.0 / (1.0 + np.exp(-v))


def setup_inputs():
    return {"table": bf(np.random.standard_normal((K, S))), "w": bf(np.random.standard_normal((D, K, M)) / np.sqrt(D * K)), "b": f32(0.5 * np.random.standard_normal((M, 1))), "offs": striped(np.random.permutation(S)[:N])}


def reference(table, w, b, offs):
    idx = offs[:16].T.reshape(-1)
    x = f64(table)[:, idx]
    y = sum(f64(w)[t].T @ x[:, t * V : (t + 1) * V] for t in range(D)) + f64(b)
    return sigmoid(y[:H]) * np.maximum(y[H:], 0.0)

@@ -1,0 +1,56 @@
+import concourse.mybir as mybir
+
+P = 128
+S, K, M = 1024, 256, 512
+ENDS, V = 2, 256
+H = M // 2
+K_BLOCKS, H_BLOCKS = K // P, H // P
+END_COLS = V // 16
+
+FLOPS = 2 * ENDS * K * M * V
+
+BF16, F32, U16 = mybir.dt.bfloat16, mybir.dt.float32, mybir.dt.uint16
+ALU = mybir.AluOpType
+ACT = mybir.ActivationFunctionType
+
+
+def tile_rows_ggate_relu_sub_kernel(tc, table, w, b, offs, out):
+    nc = tc.nc
+    with (
+        tc.tile_pool(name="held", bufs=1) as held,
+        tc.psum_pool(name="psum", bufs=1) as psum,
+    ):
+        offsets = held.tile([P, ENDS * END_COLS], U16, name="offsets")
+        nodes = [held.tile([P, S], BF16, name=f"nodes{kb}") for kb in range(K_BLOCKS)]
+        weights = [held.tile([P, ENDS, M], BF16, name=f"weights{kb}") for kb in range(K_BLOCKS)]
+        bias = held.tile([P, M // P], F32, name="bias")
+
+        nc.sync.dma_start(offsets[:], offs)
+        for kb in range(K_BLOCKS):
+            rows = slice(kb * P, (kb + 1) * P)
+            nc.sync.dma_start(nodes[kb][:], table[rows, :])
+            nc.scalar.dma_start(weights[kb][:], w[:, rows, :].rearrange("t k m -> k t m"))
+        nc.scalar.dma_start(bias[:], b.rearrange("(a p) o -> p (a o)", p=P))
+
+        sums = [psum.tile([P, V], F32, name=f"sums{mb}") for mb in range(M // P)]
+        for kb in range(K_BLOCKS):
+            for hb in range(H_BLOCKS):
+                for mb in (hb, H_BLOCKS + hb):
+                    for end in range(ENDS):
+                        nc.tensor.matmul(
+                            sums[mb][:],
+                            weights[kb][:, end, mb * P : (mb + 1) * P],
+                            nodes[kb][:].indirect(offsets[:, end * END_COLS : (end + 1) * END_COLS]),
+                            start=(kb == 0 and end == 0),
+                            stop=(kb == K_BLOCKS - 1 and end == ENDS - 1),
+                        )
+
+        for hb in range(H_BLOCKS):
+            mb = H_BLOCKS + hb
+            gate = held.tile([P, V], F32, name=f"gate{hb}")
+            value = held.tile([P, V], F32, name=f"value{hb}")
+            message = held.tile([P, V], F32, name=f"message{hb}")
+            nc.scalar.activation(gate[:], sums[hb][:], ACT.Sigmoid, bias=bias[:, hb : hb + 1])
+            nc.vector.tensor_scalar(value[:], sums[mb][:], bias[:, mb : mb + 1], 0.0, ALU.add, ALU.max)
+            nc.vector.tensor_tensor(message[:], gate[:], value[:], ALU.mult)
+            nc.sync.dma_start(out[hb * P : (hb + 1) * P, :], message[:])

@@ -25,32 +25,39 @@ def tile_rows_ggate_relu_sub_kernel(tc, table, w, b, offs, out):
         weights = [held.tile([P, ENDS, M], BF16, name=f"weights{kb}") for kb in range(K_BLOCKS)]
         bias = held.tile([P, M // P], F32, name="bias")
 
+        nc.sync.dma_start(nodes[0][:], table[:P, :])
+        nc.sync.dma_start(weights[0][:, 0, :], w[0, :P, :])
         nc.sync.dma_start(offsets[:], offs)
-        for kb in range(K_BLOCKS):
-            rows = slice(kb * P, (kb + 1) * P)
-            nc.sync.dma_start(nodes[kb][:], table[rows, :])
-            nc.scalar.dma_start(weights[kb][:], w[:, rows, :].rearrange("t k m -> k t m"))
-        nc.scalar.dma_start(bias[:], b.rearrange("(a p) o -> p (a o)", p=P))
+        nc.sync.dma_start(weights[0][:, 1, :], w[1, :P, :])
+        nc.sync.dma_start(bias[:], b.rearrange("(a p) o -> p (a o)", p=P))
+        nc.sync.dma_start(nodes[1][:], table[P:, :])
+        nc.sync.dma_start(weights[1][:], w[:, P:, :].rearrange("t k m -> k t m"))
 
         sums = [psum.tile([P, V], F32, name=f"sums{mb}") for mb in range(M // P)]
-        for kb in range(K_BLOCKS):
-            for hb in range(H_BLOCKS):
-                for mb in (hb, H_BLOCKS + hb):
-                    for end in range(ENDS):
-                        nc.tensor.matmul(
-                            sums[mb][:],
-                            weights[kb][:, end, mb * P : (mb + 1) * P],
-                            nodes[kb][:].indirect(offsets[:, end * END_COLS : (end + 1) * END_COLS]),
-                            start=(kb == 0 and end == 0),
-                            stop=(kb == K_BLOCKS - 1 and end == ENDS - 1),
-                        )
+
+        def gathered_matmul(kb, end, mb):
+            nc.tensor.matmul(
+                sums[mb][:],
+                weights[kb][:, end, mb * P : (mb + 1) * P],
+                nodes[kb][:].indirect(offsets[:, end * END_COLS : (end + 1) * END_COLS]),
+                start=(kb == 0 and end == 0),
+                stop=(kb == K_BLOCKS - 1 and end == ENDS - 1),
+            )
+
+        for end in range(ENDS):
+            for mb in range(M // P):
+                gathered_matmul(0, end, mb)
+        for hb in range(H_BLOCKS):
+            for mb in (hb, H_BLOCKS + hb):
+                for end in range(ENDS):
+                    gathered_matmul(1, end, mb)
 
         for hb in range(H_BLOCKS):
             mb = H_BLOCKS + hb
             gate = held.tile([P, V], F32, name=f"gate{hb}")
-            value = held.tile([P, V], F32, name=f"value{hb}")
+            gated = held.tile([P, V], F32, name=f"gated{hb}")
             message = held.tile([P, V], F32, name=f"message{hb}")
             nc.scalar.activation(gate[:], sums[hb][:], ACT.Sigmoid, bias=bias[:, hb : hb + 1])
-            nc.vector.tensor_scalar(value[:], sums[mb][:], bias[:, mb : mb + 1], 0.0, ALU.add, ALU.max)
-            nc.vector.tensor_tensor(message[:], gate[:], value[:], ALU.mult)
+            nc.vector.scalar_tensor_tensor(gated[:], sums[mb][:], bias[:, mb : mb + 1], gate[:], ALU.add, ALU.mult)
+            nc.vector.tensor_scalar_max(message[:], gated[:], 0.0)
             nc.sync.dma_start(out[hb * P : (hb + 1) * P, :], message[:])

@@ -4,8 +4,9 @@ P = 128
 S, K, M = 1024, 256, 512
 ENDS, V = 2, 256
 H = M // 2
-K_BLOCKS, H_BLOCKS = K // P, H // P
+K_BLOCKS, M_BLOCKS, H_BLOCKS = K // P, M // P, H // P
 END_COLS = V // 16
+QUAD = 32
 
 FLOPS = 2 * ENDS * K * M * V
 
@@ -23,17 +24,24 @@ def tile_rows_ggate_relu_sub_kernel(tc, table, w, b, offs, out):
         offsets = held.tile([P, ENDS * END_COLS], U16, name="offsets")
         nodes = [held.tile([P, S], BF16, name=f"nodes{kb}") for kb in range(K_BLOCKS)]
         weights = [held.tile([P, ENDS, M], BF16, name=f"weights{kb}") for kb in range(K_BLOCKS)]
-        bias = held.tile([P, M // P], F32, name="bias")
+
+        bias_rows = held.tile([P, M_BLOCKS * QUAD], F32, name="bias_rows", align_bytes=64)
+        bias = held.tile([P, M_BLOCKS * QUAD], F32, name="bias", align_bytes=64)
+        nc.vector.memset(bias_rows[:], 0.0)
+        nc.scalar.dma_start(
+            bias_rows[::QUAD, :].rearrange("q (a j) -> q a j", j=QUAD),
+            b.rearrange("(a q j) o -> q a (j o)", a=M_BLOCKS, j=QUAD),
+        )
+        nc.vector.transpose(bias[:], bias_rows[:])
 
         nc.sync.dma_start(nodes[0][:], table[:P, :])
         nc.sync.dma_start(weights[0][:, 0, :], w[0, :P, :])
         nc.sync.dma_start(offsets[:], offs)
         nc.sync.dma_start(weights[0][:, 1, :], w[1, :P, :])
-        nc.sync.dma_start(bias[:], b.rearrange("(a p) o -> p (a o)", p=P))
         nc.sync.dma_start(nodes[1][:], table[P:, :])
         nc.sync.dma_start(weights[1][:], w[:, P:, :].rearrange("t k m -> k t m"))
 
-        sums = [psum.tile([P, V], F32, name=f"sums{mb}") for mb in range(M // P)]
+        sums = [psum.tile([P, V], F32, name=f"sums{mb}") for mb in range(M_BLOCKS)]
 
         def gathered_matmul(kb, end, mb):
             nc.tensor.matmul(
@@ -45,19 +53,22 @@ def tile_rows_ggate_relu_sub_kernel(tc, table, w, b, offs, out):
             )
 
         for end in range(ENDS):
-            for mb in range(M // P):
+            for mb in range(M_BLOCKS):
                 gathered_matmul(0, end, mb)
         for hb in range(H_BLOCKS):
             for mb in (hb, H_BLOCKS + hb):
                 for end in range(ENDS):
                     gathered_matmul(1, end, mb)
 
+        def bias_of(mb):
+            return bias[:, QUAD * mb : QUAD * mb + 1]
+
         for hb in range(H_BLOCKS):
             mb = H_BLOCKS + hb
             gate = held.tile([P, V], F32, name=f"gate{hb}")
             gated = held.tile([P, V], F32, name=f"gated{hb}")
             message = held.tile([P, V], F32, name=f"message{hb}")
-            nc.scalar.activation(gate[:], sums[hb][:], ACT.Sigmoid, bias=bias[:, hb : hb + 1])
-            nc.vector.scalar_tensor_tensor(gated[:], sums[mb][:], bias[:, mb : mb + 1], gate[:], ALU.add, ALU.mult)
+            nc.scalar.activation(gate[:], sums[hb][:], ACT.Sigmoid, bias=bias_of(hb))
+            nc.vector.scalar_tensor_tensor(gated[:], sums[mb][:], bias_of(mb), gate[:], ALU.add, ALU.mult)
             nc.vector.tensor_scalar_max(message[:], gated[:], 0.0)
             nc.sync.dma_start(out[hb * P : (hb + 1) * P, :], message[:])

@@ -25,6 +25,14 @@ def tile_rows_ggate_relu_sub_kernel(tc, table, w, b, offs, out):
         nodes = [held.tile([P, S], BF16, name=f"nodes{kb}") for kb in range(K_BLOCKS)]
         weights = [held.tile([P, ENDS, M], BF16, name=f"weights{kb}") for kb in range(K_BLOCKS)]
 
+        nc.sync.dma_start(nodes[0][:], table[:P, :])
+        nc.scalar.dma_start(weights[0][:, 0, :H], w[0, :P, :H])
+        nc.sync.dma_start(offsets[:], offs)
+        nc.sync.dma_start(weights[0][:, 0, H:], w[0, :P, H:])
+        nc.sync.dma_start(weights[0][:, 1, :], w[1, :P, :])
+        nc.sync.dma_start(nodes[1][:], table[P:, :])
+        nc.sync.dma_start(weights[1][:], w[:, P:, :].rearrange("t k m -> k t m"))
+
         bias_rows = held.tile([P, M_BLOCKS * QUAD], F32, name="bias_rows", align_bytes=64)
         bias = held.tile([P, M_BLOCKS * QUAD], F32, name="bias", align_bytes=64)
         nc.vector.memset(bias_rows[:], 0.0)
@@ -33,13 +41,6 @@ def tile_rows_ggate_relu_sub_kernel(tc, table, w, b, offs, out):
             b.rearrange("(a q j) o -> q a (j o)", a=M_BLOCKS, j=QUAD),
         )
         nc.vector.transpose(bias[:], bias_rows[:])
-
-        nc.sync.dma_start(nodes[0][:], table[:P, :])
-        nc.sync.dma_start(weights[0][:, 0, :], w[0, :P, :])
-        nc.sync.dma_start(offsets[:], offs)
-        nc.sync.dma_start(weights[0][:, 1, :], w[1, :P, :])
-        nc.sync.dma_start(nodes[1][:], table[P:, :])
-        nc.sync.dma_start(weights[1][:], w[:, P:, :].rearrange("t k m -> k t m"))
 
         sums = [psum.tile([P, V], F32, name=f"sums{mb}") for mb in range(M_BLOCKS)]
 

import concourse.mybir as mybir

P = 128
S, K, M = 1024, 256, 512
ENDS, V = 2, 256
H = M // 2
K_BLOCKS, M_BLOCKS, H_BLOCKS = K // P, M // P, H // P
END_COLS = V // 16
QUAD = 32

FLOPS = 2 * ENDS * K * M * V

BF16, F32, U16 = mybir.dt.bfloat16, mybir.dt.float32, mybir.dt.uint16
ALU = mybir.AluOpType
ACT = mybir.ActivationFunctionType


def tile_rows_ggate_relu_sub_kernel(tc, table, w, b, offs, out):
    nc = tc.nc
    with (
        tc.tile_pool(name="held", bufs=1) as held,
        tc.psum_pool(name="psum", bufs=1) as psum,
    ):
        offsets = held.tile([P, ENDS * END_COLS], U16, name="offsets")
        nodes = [held.tile([P, S], BF16, name=f"nodes{kb}") for kb in range(K_BLOCKS)]
        weights = [held.tile([P, ENDS, M], BF16, name=f"weights{kb}") for kb in range(K_BLOCKS)]

        nc.sync.dma_start(nodes[0][:], table[:P, :])
        nc.scalar.dma_start(weights[0][:, 0, :H], w[0, :P, :H])
        nc.sync.dma_start(offsets[:], offs)
        nc.sync.dma_start(weights[0][:, 0, H:], w[0, :P, H:])
        nc.sync.dma_start(weights[0][:, 1, :], w[1, :P, :])
        nc.sync.dma_start(nodes[1][:], table[P:, :])
        nc.sync.dma_start(weights[1][:], w[:, P:, :].rearrange("t k m -> k t m"))

        bias_rows = held.tile([P, M_BLOCKS * QUAD], F32, name="bias_rows", align_bytes=64)
        bias = held.tile([P, M_BLOCKS * QUAD], F32, name="bias", align_bytes=64)
        nc.vector.memset(bias_rows[:], 0.0)
        nc.scalar.dma_start(
            bias_rows[::QUAD, :].rearrange("q (a j) -> q a j", j=QUAD),
            b.rearrange("(a q j) o -> q a (j o)", a=M_BLOCKS, j=QUAD),
        )
        nc.vector.transpose(bias[:], bias_rows[:])

        sums = [psum.tile([P, V], F32, name=f"sums{mb}") for mb in range(M_BLOCKS)]

        def gathered_matmul(kb, end, mb):
            nc.tensor.matmul(
                sums[mb][:],
                weights[kb][:, end, mb * P : (mb + 1) * P],
                nodes[kb][:].indirect(offsets[:, end * END_COLS : (end + 1) * END_COLS]),
                start=(kb == 0 and end == 0),
                stop=(kb == K_BLOCKS - 1 and end == ENDS - 1),
            )

        for end in range(ENDS):
            for mb in range(M_BLOCKS):
                gathered_matmul(0, end, mb)
        for hb in range(H_BLOCKS):
            for mb in (hb, H_BLOCKS + hb):
                for end in range(ENDS):
                    gathered_matmul(1, end, mb)

        def bias_of(mb):
            return bias[:, QUAD * mb : QUAD * mb + 1]

        for hb in range(H_BLOCKS):
            mb = H_BLOCKS + hb
            gate = held.tile([P, V], F32, name=f"gate{hb}")
            gated = held.tile([P, V], F32, name=f"gated{hb}")
            message = held.tile([P, V], F32, name=f"message{hb}")
            nc.scalar.activation(gate[:], sums[hb][:], ACT.Sigmoid, bias=bias_of(hb))
            nc.vector.scalar_tensor_tensor(gated[:], sums[mb][:], bias_of(mb), gate[:], ALU.add, ALU.mult)
            nc.vector.tensor_scalar_max(message[:], gated[:], 0.0)
            nc.sync.dma_start(out[hb * P : (hb + 1) * P, :], message[:])
